import numpy as np
import ml_dtypes


def mxq(x, axis, fmt="e4m3"):
    dtype, down = {"e4m3": (ml_dtypes.float8_e4m3fn, 7), "e5m2": (ml_dtypes.float8_e5m2, 14)}[fmt]
    v = np.moveaxis(np.asarray(x, np.float32).astype(ml_dtypes.bfloat16).astype(np.float64), axis, -1)
    blocks = v.reshape(v.shape[:-1] + (-1, 32))
    amax = np.abs(blocks).max(-1, keepdims=True)
    byte = np.maximum(np.where(amax > 0, np.frexp(amax)[1] - 1 + 127, 0) - down, 1)
    scale = np.exp2(byte - 127.0)
    codes = (blocks / scale).astype(np.float32).astype(dtype).astype(np.float64)
    return np.moveaxis((codes * scale).reshape(v.shape), -1, axis)


WIDE = False


def mx_kscale(k):
    if not WIDE:
        return np.ones(k)
    levels = np.array([10, -10, 5, -5, 0])
    if k % 512:
        return np.exp2(np.random.permutation(np.resize(levels, k // 32))).repeat(32)
    a = np.empty((k // 512, 16))
    for p in range(k // 512):
        a[p, :8] = np.random.permutation(np.resize(levels, 8))
        for g in range(8):
            far = levels[np.abs(levels - a[p, g]) >= 10]
            a[p, g + 8] = far[np.random.randint(len(far))]
    return np.exp2(a.ravel()).repeat(32)


def f64(x):
    return np.asarray(x).astype(np.float64)


def striped(idx):
    return np.tile(idx.reshape(-1, 16).T, (8, 1)).astype(np.uint16)


def unstriped(offs):
    return offs[:16].T.reshape(-1).astype(np.int64)


def striped8(idx):
    return np.concatenate([x.reshape(-1, 16).T for x in idx]).astype(np.uint16)


def runs(offs, k):
    lists = np.stack([offs[16 * r : 16 * r + 16].T.reshape(-1) for r in range(8)]).astype(np.int64)
    return lists[np.arange(k) % 512 // 64]


def pack_weight(w):
    k, n = w.shape
    w = f64(np.asarray(w, np.float32).astype(ml_dtypes.bfloat16)).reshape(k // 32, 32, n)
    amax = np.abs(w).max(1)
    byte = np.clip(np.where(amax > 0, np.frexp(amax)[1] - 1 + 127 - 7, 1), 1, 254)
    scaled = (w * np.exp2(127.0 - byte)[:, None, :]).reshape(k, n).astype(np.float32)
    words = np.ascontiguousarray(scaled.reshape(k // 512, 128, 4, n).transpose(0, 1, 3, 2)).astype(ml_dtypes.float8_e4m3fn).view(np.uint8)
    return words, np.ascontiguousarray(byte.astype(np.uint8).reshape(k // 512, 16, n))


def unpack_weight(words, scales):
    g, p, n, _ = words.shape
    vals = np.ascontiguousarray(words).view(ml_dtypes.float8_e4m3fn).astype(np.float64) * np.repeat(np.exp2(scales.astype(np.float64) - 127.0), 8, axis=1)[..., None]
    return vals.transpose(0, 1, 3, 2).reshape(g * 512, n)


def sigmoid(v):
    return 1.0 / (1.0 + np.exp(-np.maximum(v, -700.0)))


K, T, S, N, H, W = 512, 2048, 512, 512, 512, 256


def setup_inputs():
    n = np.random.standard_normal
    s = mx_kscale(K)[:, None]
    u = mx_kscale(H)
    packed_xT = pack_weight(n((K, T)) * s)
    perm = np.stack([np.random.permutation(S) for _ in range(8)])
    return {
        "x_words": packed_xT[0],
        "x_scales": packed_xT[1],
        "w1": (n((K, H)) / np.sqrt(K) / s).astype(np.float32),
        "gn": (np.random.uniform(0.5, 1.5, (H, 1)) * u[:, None]).astype(np.float32),
        "w2": (n((H, N)) / np.sqrt(H) / u[:, None]).astype(np.float32),
        "gm": (np.random.uniform(0.5, 1.5, (H, 1)) * u[:, None]).astype(np.float32),
        "w3": (n((H, N)) / np.sqrt(H) / u[:, None]).astype(np.float32),
        "offs": striped(np.random.permutation(T)[:S]),
        "n1": striped8(perm[:, :W]),
        "n2": striped8(perm[:, W:]),
        "n3": striped8(np.stack([np.random.permutation(S) for _ in range(8)])),
        "n4": striped8(np.stack([np.random.permutation(S) for _ in range(8)])),
        "n5": striped8(np.stack([np.random.permutation(S) for _ in range(8)])),
        "n6": striped8(np.stack([np.random.permutation(S) for _ in range(8)])),
        "n7": striped8(np.stack([np.random.permutation(S) for _ in range(8)])),
    }


def reference(x_words, x_scales, w1, gn, w2, gm, w3, offs, n1, n2, n3, n4, n5, n6, n7):
    xq = unpack_weight(x_words, x_scales)[:, unstriped(offs)]
    y = mxq(f64(w1), 0, "e4m3").T @ xq
    pa = y[np.arange(H)[:, None], runs(n1, H)]
    pb = y[np.arange(H)[:, None], runs(n2, H)]
    ra = pa * sigmoid(pb)
    ds = y.copy()
    ds[np.arange(H)[:, None], runs(n2, H)] = ra
    z = f64(gn) * ds
    a = mxq(f64(w2), 0, "e4m3").T @ mxq(z, 0, "e4m3")
    ex = np.exp(0.5 * y)
    z2 = f64(gm) * (np.log((ex + ex[np.arange(H)[:, None], runs(n3, H)]) / (ex[np.arange(H)[:, None], runs(n4, H)] + ex[np.arange(H)[:, None], runs(n5, H)])))
    b = mxq(f64(w3), 0, "e4m3").T @ mxq(z2, 0, "e4m3")
    return (a - (a[np.arange(N)[:, None], runs(n6, N)])) / (np.abs(b) + np.abs(b[np.arange(N)[:, None], runs(n7, N)]) + 0.5)

@@ -1,0 +1,255 @@
+from contextlib import ExitStack
+
+import concourse.mybir as mybir
+from concourse.masks import make_identity
+
+K, T, S, N, H, W = 512, 2048, 512, 512, 512, 256
+FLOPS = 2 * K * H * S + 2 * 2 * H * N * S
+
+F32 = mybir.dt.float32
+BF16 = mybir.dt.bfloat16
+I32 = mybir.dt.int32
+U32 = mybir.dt.uint32
+U16 = mybir.dt.uint16
+U8 = mybir.dt.uint8
+FP8X4 = mybir.dt.float8_e4m3fn_x4
+ACT = mybir.ActivationFunctionType
+ALU = mybir.AluOpType
+
+P = 128
+PACK = 4
+HALF = S // 2
+LCOLS = HALF // 16
+
+
+def tile_picked_forknormbfoldodds_none_p_kernel(tc, x_words, x_scales, w1, gn, w2, gm, w3, offs, n1, n2, n3, n4, n5, n6, n7, out):
+    nc = tc.nc
+    with ExitStack() as ctx:
+        lists = ctx.enter_context(tc.tile_pool(name="lists", bufs=1))
+        keep = ctx.enter_context(tc.tile_pool(name="keep", bufs=1))
+        psum = ctx.enter_context(tc.psum_pool(name="psum", bufs=1))
+
+        def sb(name, shape, dtype, tag=None):
+            return keep.tile(shape, dtype, name=name, tag=tag or name, align_bytes=64)
+
+        def bank(index, name, shape):
+            return psum.tile(shape, F32, name=name, tag="bank%d" % index)
+
+        def load_list(name, src):
+            tl = lists.tile([P, src.shape[1]], U16, name=name)
+            nc.sync.dma_start(tl[:], src)
+            return tl
+
+        def load_weight(name, src, tag):
+            raw = sb(name, [P, PACK, H], F32, tag)
+            nc.sync.dma_start(raw[:], src.rearrange("(p j) n -> p j n", j=PACK))
+            return raw
+
+        def load_gain(name, src):
+            g = sb(name, [P, PACK], F32)
+            nc.gpsimd.dma_start(g[:], src.rearrange("(p t) o -> p (t o)", t=PACK))
+            return g
+
+        def deal(raw, grouped, m0, m1, on_scalar):
+            dst = grouped[:].rearrange("p (t m j) -> p m j t", t=PACK, j=PACK)[:, m0:m1]
+            src = raw[:].rearrange("p j (m t) -> p m j t", t=PACK)[:, m0:m1]
+            if on_scalar:
+                nc.scalar.activation(out=dst, in_=src, func=ACT.Copy)
+            else:
+                nc.vector.tensor_copy(out=dst, in_=src)
+
+        def quantize(codes, scales, grouped, c0, c1):
+            nc.vector.quantize_mx(out=codes[:, c0:c1].bitcast(FP8X4), scales=scales[:, c0:c1], in_=grouped[:, PACK * c0 : PACK * c1])
+
+        def product(acc, w_codes, w_scales, t, codes, scales, c0, c1):
+            nc.tensor.matmul_mx(
+                out=acc[:, c0:c1],
+                lhsT=w_codes[:, P * t : P * (t + 1)].bitcast(FP8X4),
+                lhsT_scale=w_scales[:, P * t : P * (t + 1)],
+                rhs=codes[:, c0:c1].bitcast(FP8X4),
+                rhs_scale=scales[:, c0:c1],
+                start=True,
+                stop=True,
+            )
+
+        def gather(dst, window, lst, h, on_scalar):
+            o = dst[:, HALF * h : HALF * (h + 1)]
+            src = window[:].indirect(lst[:, LCOLS * h : LCOLS * (h + 1)])
+            if on_scalar:
+                nc.scalar.activation(out=o, in_=src, func=ACT.Copy)
+            else:
+                nc.vector.tensor_copy(out=o, in_=src)
+
+        x_sc = sb("x_sc", [P, T], U8)
+        nc.gpsimd.memset(x_sc[:].bitcast(I32), 0)
+        l_offs = load_list("l_offs", offs)
+        l3 = load_list("l3", n3)
+        l4 = load_list("l4", n4)
+        l5 = load_list("l5", n5)
+        l1 = load_list("l1", n1)
+        l2 = load_list("l2", n2)
+        w1_raw = load_weight("w1_raw", w1, "w1_raw")
+        x_w = sb("x_w", [P, T], U32)
+        nc.sync.dma_start(x_w[:].bitcast(I32), x_words[0].rearrange("p n r -> p (n r)").bitcast(I32))
+        for q in range(4):
+            nc.scalar.dma_start(x_sc[32 * q : 32 * q + 4, :].bitcast(I32), x_scales[0, 4 * q : 4 * q + 4, :].bitcast(I32))
+        gm_sb = load_gain("gm_sb", gm)
+        gn_sb = load_gain("gn_sb", gn)
+        l7 = load_list("l7", n7)
+        l6 = load_list("l6", n6)
+
+        ident = sb("ident", [P, P], F32)
+        make_identity(nc, ident[:])
+
+        xg_sc = sb("xg_sc", [P, S], U8)
+        nc.vector.tensor_copy(out=xg_sc[:], in_=x_sc[:].indirect(l_offs[:]))
+        w1_g = sb("w1_g", [P, PACK * H], BF16)
+        deal(w1_raw, w1_g, 0, 80, False)
+        deal(w1_raw, w1_g, 80, 128, True)
+        w1_c = sb("w1_c", [P, H], U32)
+        w1_s = sb("w1_s", [P, H], U8)
+        quantize(w1_c, w1_s, w1_g, 0, H)
+        w3_raw = load_weight("w3_raw", w3, "w1_raw")
+        w2_raw = load_weight("w2_raw", w2, "w1_g")
+        xg_w = sb("xg_w", [P, S], U32)
+        y_ps = [bank(t, "y_ps%d" % t, [P, S]) for t in range(PACK)]
+        for h in range(2):
+            gather(xg_w, x_w, l_offs, h, False)
+            for t in range(PACK):
+                product(y_ps[t], w1_c, w1_s, t, xg_w, xg_sc, HALF * h, HALF * (h + 1))
+
+        ex = [sb("ex%d" % t, [P, S], F32) for t in range(PACK)]
+        ds = [sb("ds%d" % t, [P, S], F32) for t in range(PACK)]
+        for t in range(PACK):
+            nc.scalar.activation(out=ex[t][:], in_=y_ps[t][:], func=ACT.Exp, scale=0.5)
+
+        w3_g = sb("w3_g", [P, PACK * N], BF16)
+        w3_c = sb("w3_c", [P, N], U32)
+        w3_s = sb("w3_s", [P, N], U8)
+        w2_c = sb("w2_c", [P, N], U32)
+        w2_s = sb("w2_s", [P, N], U8)
+
+        odds = []
+        got = []
+        for t in range(PACK):
+            e3 = sb("e3_%d" % t, [P, S], F32)
+            e4 = sb("e4_%d" % t, [P, S], F32)
+            e5 = sb("e5_%d" % t, [P, S], F32)
+            got.append((e3, e4, e5))
+            for h in range(2):
+                gather(e3, ex[t], l3, h, False)
+            for h in range(2):
+                gather(e4, ex[t], l4, h, False)
+            for h in range(2):
+                gather(e5, ex[t], l5, h, t > 0 or h == 1)
+        for t in range(PACK):
+            nc.scalar.copy(out=ds[t][:], in_=y_ps[t][:])
+        for t in range(PACK):
+            e3, e4, e5 = got[t]
+            top = bank((4 + 2 * t) % 8, "top%d" % t, [P, 4, P])
+            bot = bank((5 + 2 * t) % 8, "bot%d" % t, [P, 4, P])
+            for acc, first, second in ((top, e3, ex[t]), (bot, e5, e4)):
+                for c in range(4):
+                    cols = slice(P * c, P * (c + 1))
+                    nc.tensor.matmul(acc[:, c, :], first[:, cols], ident[:], is_transpose=True, start=True, stop=False)
+                    nc.tensor.matmul(acc[:, c, :], second[:, cols], ident[:], is_transpose=True, start=False, stop=True)
+            ln_top = sb("ln_top%d" % t, [P, 4, P], F32)
+            ln_bot = sb("ln_bot%d" % t, [P, 4, P], F32)
+            nc.scalar.activation(out=ln_top[:], in_=top[:], func=ACT.Ln)
+            nc.scalar.activation(out=ln_bot[:], in_=bot[:], func=ACT.Ln)
+            odds.append(sb("odds%d" % t, [P, 4, P], F32))
+            nc.vector.tensor_tensor(out=odds[t][:], in0=ln_top[:], in1=ln_bot[:], op=ALU.subtract)
+            if t == 1:
+                for m0 in range(0, P, 32):
+                    deal(w3_raw, w3_g, m0, m0 + 32, False)
+                quantize(w3_c, w3_s, w3_g, 0, N)
+
+        back = [bank(3 - c, "back%d" % c, [P, PACK, P]) for c in range(4)]
+        for c in range(4):
+            for t in range(PACK):
+                nc.tensor.transpose(back[c][:, t, :], odds[t][:, c, :], ident[:])
+        z2_g = sb("z2_g", [P, PACK * S], BF16)
+        z2_c = sb("z2_c", [P, S], U32)
+        z2_s = sb("z2_s", [P, S], U8)
+        b_ps = [bank(4 + t, "b_ps%d" % t, [P, S]) for t in range(PACK)]
+        for h in range(2):
+            for c in (2 * h, 2 * h + 1):
+                nc.vector.tensor_tensor(
+                    out=z2_g[:, PACK * P * c : PACK * P * (c + 1)].rearrange("p (j t) -> p j t", t=PACK),
+                    in0=back[c][:].rearrange("p t j -> p j t"),
+                    in1=gm_sb[:].unsqueeze(1).to_broadcast([P, P, PACK]),
+                    op=ALU.mult,
+                )
+            quantize(z2_c, z2_s, z2_g, HALF * h, HALF * (h + 1))
+            for t in range(PACK):
+                product(b_ps[t], w3_c, w3_s, t, z2_c, z2_s, HALF * h, HALF * (h + 1))
+
+        w2_g = sb("w2_g", [P, PACK * N], BF16, "odds3")
+        for m0 in range(0, P, 32):
+            deal(w2_raw, w2_g, m0, m0 + 32, False)
+        quantize(w2_c, w2_s, w2_g, 0, N)
+        z_planes = sb("z_planes", [P, PACK, S], BF16)
+        gates = [sb("gates01", [P, 2, W], F32, "ln_bot3"), sb("gates23", [P, 2, W], F32, "ln_top3")]
+        for t in range(PACK):
+            pa = sb("pa%d" % t, [P, W], F32)
+            gate = gates[t // 2][:, t % 2, :]
+            nc.scalar.activation(out=gate, in_=ds[t][:].indirect(l2[:]), func=ACT.Sigmoid)
+            nc.scalar.activation(out=pa[:], in_=ds[t][:].indirect(l1[:]), func=ACT.Copy)
+            nc.vector.tensor_tensor(out=ds[t][:].indirect(l2[:]), in0=pa[:], in1=gate, op=ALU.mult)
+            nc.vector.tensor_scalar(out=z_planes[:, t, :], in0=ds[t][:], scalar1=gn_sb[:, t : t + 1], scalar2=None, op0=ALU.mult)
+        dens = []
+        for t in range(PACK):
+            size = sb("size%d" % t, [P, S], F32)
+            nc.scalar.activation(out=size[:], in_=b_ps[t][:], func=ACT.Abs)
+            s7 = sb("s7_%d" % t, [P, S], F32)
+            for h in range(2):
+                gather(s7, size, l7, h, True)
+            den = bank(4 + t, "den%d" % t, [P, 4, P])
+            for c in range(4):
+                cols = slice(P * c, P * (c + 1))
+                nc.tensor.matmul(den[:, c, :], size[:, cols], ident[:], is_transpose=True, start=True, stop=False)
+                nc.tensor.matmul(den[:, c, :], s7[:, cols], ident[:], is_transpose=True, start=False, stop=True)
+            dens.append(den)
+
+        z_g = sb("z_g", [P, PACK * S], BF16)
+        z_c = sb("z_c", [P, S], U32, "s7_2")
+        z_s = sb("z_s", [P, S], U8)
+        a_ps = [bank(t, "a_ps%d" % t, [P, S]) for t in range(PACK)]
+        for h in range(2):
+            nc.vector.tensor_copy(
+                out=z_g[:, PACK * HALF * h : PACK * HALF * (h + 1)].rearrange("p (c i t) -> p c t i", i=4, t=PACK),
+                in_=z_planes[:, :, HALF * h : HALF * (h + 1)].rearrange("p t (c i) -> p c t i", i=4),
+            )
+            quantize(z_c, z_s, z_g, HALF * h, HALF * (h + 1))
+            for t in range(PACK):
+                product(a_ps[t], w2_c, w2_s, t, z_c, z_s, HALF * h, HALF * (h + 1))
+
+        a_tags = ["size2", "size3", "s7_3", "root0"]
+        a_sb = [None] * PACK
+        inv = []
+        for t in range(PACK):
+            if t < 2:
+                a_sb[t] = sb("a_sb%d" % t, [P, S], F32, a_tags[t])
+                nc.scalar.copy(out=a_sb[t][:], in_=a_ps[t][:])
+            root = sb("root%d" % t, [P, 4, P], F32)
+            nc.scalar.activation(out=root[:], in_=dens[t][:], func=ACT.Abs_reciprocal_sqrt, bias=0.5)
+            sq = sb("sq%d" % t, [P, 4, P], F32)
+            nc.scalar.activation(out=sq[:], in_=root[:], func=ACT.Square)
+            r = bank(4 + t, "inv%d" % t, [P, S])
+            for c in range(4):
+                nc.tensor.transpose(r[:, P * c : P * (c + 1)], sq[:, c, :], ident[:])
+            inv.append(r)
+            if t < 2:
+                a_sb[t + 2] = sb("a_sb%d" % (t + 2), [P, S], F32, a_tags[t + 2])
+                nc.scalar.copy(out=a_sb[t + 2][:], in_=a_ps[t + 2][:])
+
+        out_rows = out.rearrange("(p t) n -> t p n", t=PACK)
+        for t in range(PACK):
+            a6 = sb("a6_%d" % t, [P, S], F32)
+            for h in range(2):
+                gather(a6, a_sb[t], l6, h, t == 3 or (t == 2 and h == 1))
+            diff = sb("diff%d" % t, [P, S], F32)
+            nc.vector.tensor_tensor(out=diff[:], in0=a_ps[t][:], in1=a6[:], op=ALU.subtract)
+            res = sb("res%d" % t, [P, S], F32)
+            nc.vector.tensor_tensor(out=res[:], in0=inv[t][:], in1=diff[:], op=ALU.mult)
+            nc.sync.dma_start(out_rows[t], res[:])

@@ -20,6 +20,9 @@ P = 128
 PACK = 4
 HALF = S // 2
 LCOLS = HALF // 16
+SQ_V = (0, 1, 2)
+A6_S = 4
+E5_S = 1
 
 
 def tile_picked_forknormbfoldodds_none_p_kernel(tc, x_words, x_scales, w1, gn, w2, gm, w3, offs, n1, n2, n3, n4, n5, n6, n7, out):
@@ -45,9 +48,9 @@ def tile_picked_forknormbfoldodds_none_p_kernel(tc, x_words, x_scales, w1, gn, w
             nc.sync.dma_start(raw[:], src.rearrange("(p j) n -> p j n", j=PACK))
             return raw
 
-        def load_gain(name, src):
-            g = sb(name, [P, PACK], F32)
-            nc.gpsimd.dma_start(g[:], src.rearrange("(p t) o -> p (t o)", t=PACK))
+        def load_gain(name, src, tag):
+            g = sb(name, [P, PACK], F32, tag)
+            nc.sync.dma_start(g[:], src.rearrange("(p t) o -> p (t o)", t=PACK))
             return g
 
         def deal(raw, grouped, m0, m1, on_scalar):
@@ -72,56 +75,65 @@ def tile_picked_forknormbfoldodds_none_p_kernel(tc, x_words, x_scales, w1, gn, w
                 stop=True,
             )
 
-        def gather(dst, window, lst, h, on_scalar):
-            o = dst[:, HALF * h : HALF * (h + 1)]
-            src = window[:].indirect(lst[:, LCOLS * h : LCOLS * (h + 1)])
+        def gather(dst, window, lst, h, on_scalar, halves=1):
+            o = dst[:, HALF * h : HALF * (h + halves)]
+            src = window[:].indirect(lst[:, LCOLS * h : LCOLS * (h + halves)])
             if on_scalar:
                 nc.scalar.activation(out=o, in_=src, func=ACT.Copy)
             else:
                 nc.vector.tensor_copy(out=o, in_=src)
 
+        def gather_row(dst, window, lst, t, scalar_from):
+            if 2 * t + 1 == scalar_from:
+                gather(dst, window, lst, 0, False)
+                gather(dst, window, lst, 1, True)
+            else:
+                gather(dst, window, lst, 0, 2 * t >= scalar_from, 2)
+
         x_sc = sb("x_sc", [P, T], U8)
         nc.gpsimd.memset(x_sc[:].bitcast(I32), 0)
+        w1_raw = load_weight("w1_raw", w1, "w1_raw")
         l_offs = load_list("l_offs", offs)
         l3 = load_list("l3", n3)
         l4 = load_list("l4", n4)
         l5 = load_list("l5", n5)
         l1 = load_list("l1", n1)
         l2 = load_list("l2", n2)
-        w1_raw = load_weight("w1_raw", w1, "w1_raw")
         x_w = sb("x_w", [P, T], U32)
         nc.sync.dma_start(x_w[:].bitcast(I32), x_words[0].rearrange("p n r -> p (n r)").bitcast(I32))
         for q in range(4):
             nc.scalar.dma_start(x_sc[32 * q : 32 * q + 4, :].bitcast(I32), x_scales[0, 4 * q : 4 * q + 4, :].bitcast(I32))
-        gm_sb = load_gain("gm_sb", gm)
-        gn_sb = load_gain("gn_sb", gn)
         l7 = load_list("l7", n7)
         l6 = load_list("l6", n6)
 
         ident = sb("ident", [P, P], F32)
         make_identity(nc, ident[:])
+        win = [sb("win%d" % t, [P, 2 * S], F32) for t in range(PACK)]
+        for t in range(PACK):
+            nc.gpsimd.memset(win[t][:, S:], 0.0)
 
         xg_sc = sb("xg_sc", [P, S], U8)
         nc.vector.tensor_copy(out=xg_sc[:], in_=x_sc[:].indirect(l_offs[:]))
         w1_g = sb("w1_g", [P, PACK * H], BF16)
-        deal(w1_raw, w1_g, 0, 80, False)
-        deal(w1_raw, w1_g, 80, 128, True)
-        w1_c = sb("w1_c", [P, H], U32)
+        deal(w1_raw, w1_g, 0, 56, False)
+        deal(w1_raw, w1_g, 56, 128, True)
+        w1_c = sb("w1_c", [P, H], U32, "x_sc")
         w1_s = sb("w1_s", [P, H], U8)
         quantize(w1_c, w1_s, w1_g, 0, H)
         w3_raw = load_weight("w3_raw", w3, "w1_raw")
-        w2_raw = load_weight("w2_raw", w2, "w1_g")
-        xg_w = sb("xg_w", [P, S], U32)
+        xg_w = sb("xg_w", [P, S], U32, "w1_g")
         y_ps = [bank(t, "y_ps%d" % t, [P, S]) for t in range(PACK)]
         for h in range(2):
             gather(xg_w, x_w, l_offs, h, False)
             for t in range(PACK):
                 product(y_ps[t], w1_c, w1_s, t, xg_w, xg_sc, HALF * h, HALF * (h + 1))
 
-        ex = [sb("ex%d" % t, [P, S], F32) for t in range(PACK)]
+        w2_raw = load_weight("w2_raw", w2, "w1_g")
+        gm_sb = load_gain("gm_sb", gm, "w1_s")
+        gn_sb = load_gain("gn_sb", gn, "xg_sc")
         ds = [sb("ds%d" % t, [P, S], F32) for t in range(PACK)]
         for t in range(PACK):
-            nc.scalar.activation(out=ex[t][:], in_=y_ps[t][:], func=ACT.Exp, scale=0.5)
+            nc.scalar.activation(out=win[t][:, :S], in_=y_ps[t][:], func=ACT.Exp, scale=0.5)
 
         w3_g = sb("w3_g", [P, PACK * N], BF16)
         w3_c = sb("w3_c", [P, N], U32)
@@ -136,19 +148,16 @@ def tile_picked_forknormbfoldodds_none_p_kernel(tc, x_words, x_scales, w1, gn, w
             e4 = sb("e4_%d" % t, [P, S], F32)
             e5 = sb("e5_%d" % t, [P, S], F32)
             got.append((e3, e4, e5))
-            for h in range(2):
-                gather(e3, ex[t], l3, h, False)
-            for h in range(2):
-                gather(e4, ex[t], l4, h, False)
-            for h in range(2):
-                gather(e5, ex[t], l5, h, t > 0 or h == 1)
+            gather_row(e3, win[t], l3, t, 8)
+            gather_row(e4, win[t], l4, t, 8)
+            gather_row(e5, win[t], l5, t, E5_S)
         for t in range(PACK):
             nc.scalar.copy(out=ds[t][:], in_=y_ps[t][:])
         for t in range(PACK):
             e3, e4, e5 = got[t]
             top = bank((4 + 2 * t) % 8, "top%d" % t, [P, 4, P])
             bot = bank((5 + 2 * t) % 8, "bot%d" % t, [P, 4, P])
-            for acc, first, second in ((top, e3, ex[t]), (bot, e5, e4)):
+            for acc, first, second in ((top, e3, win[t]), (bot, e5, e4)):
                 for c in range(4):
                     cols = slice(P * c, P * (c + 1))
                     nc.tensor.matmul(acc[:, c, :], first[:, cols], ident[:], is_transpose=True, start=True, stop=False)
@@ -184,31 +193,30 @@ def tile_picked_forknormbfoldodds_none_p_kernel(tc, x_words, x_scales, w1, gn, w
             for t in range(PACK):
                 product(b_ps[t], w3_c, w3_s, t, z2_c, z2_s, HALF * h, HALF * (h + 1))
 
-        w2_g = sb("w2_g", [P, PACK * N], BF16, "odds3")
+        w2_g = sb("w2_g", [P, PACK * N], BF16, "ln_top3")
         for m0 in range(0, P, 32):
             deal(w2_raw, w2_g, m0, m0 + 32, False)
         quantize(w2_c, w2_s, w2_g, 0, N)
         z_planes = sb("z_planes", [P, PACK, S], BF16)
-        gates = [sb("gates01", [P, 2, W], F32, "ln_bot3"), sb("gates23", [P, 2, W], F32, "ln_top3")]
+        gates = sb("gates", [P, PACK, W], F32, "ln_bot3")
         for t in range(PACK):
             pa = sb("pa%d" % t, [P, W], F32)
-            gate = gates[t // 2][:, t % 2, :]
+            gate = gates[:, t, :]
             nc.scalar.activation(out=gate, in_=ds[t][:].indirect(l2[:]), func=ACT.Sigmoid)
             nc.scalar.activation(out=pa[:], in_=ds[t][:].indirect(l1[:]), func=ACT.Copy)
             nc.vector.tensor_tensor(out=ds[t][:].indirect(l2[:]), in0=pa[:], in1=gate, op=ALU.mult)
             nc.vector.tensor_scalar(out=z_planes[:, t, :], in0=ds[t][:], scalar1=gn_sb[:, t : t + 1], scalar2=None, op0=ALU.mult)
         dens = []
         for t in range(PACK):
-            size = sb("size%d" % t, [P, S], F32)
-            nc.scalar.activation(out=size[:], in_=b_ps[t][:], func=ACT.Abs)
+            size = win[t]
+            nc.scalar.activation(out=size[:, :S], in_=b_ps[t][:], func=ACT.Abs)
             s7 = sb("s7_%d" % t, [P, S], F32)
-            for h in range(2):
-                gather(s7, size, l7, h, True)
+            gather_row(s7, size, l7, t, 0)
             den = bank(4 + t, "den%d" % t, [P, 4, P])
             for c in range(4):
                 cols = slice(P * c, P * (c + 1))
-                nc.tensor.matmul(den[:, c, :], size[:, cols], ident[:], is_transpose=True, start=True, stop=False)
-                nc.tensor.matmul(den[:, c, :], s7[:, cols], ident[:], is_transpose=True, start=False, stop=True)
+                nc.tensor.matmul(den[:, c, :], s7[:, cols], ident[:], is_transpose=True, start=True, stop=False)
+                nc.tensor.matmul(den[:, c, :], size[:, cols], ident[:], is_transpose=True, start=False, stop=True)
             dens.append(den)
 
         z_g = sb("z_g", [P, PACK * S], BF16)
@@ -224,32 +232,33 @@ def tile_picked_forknormbfoldodds_none_p_kernel(tc, x_words, x_scales, w1, gn, w
             for t in range(PACK):
                 product(a_ps[t], w2_c, w2_s, t, z_c, z_s, HALF * h, HALF * (h + 1))
 
-        a_tags = ["size2", "size3", "s7_3", "root0"]
-        a_sb = [None] * PACK
         inv = []
         for t in range(PACK):
             if t < 2:
-                a_sb[t] = sb("a_sb%d" % t, [P, S], F32, a_tags[t])
-                nc.scalar.copy(out=a_sb[t][:], in_=a_ps[t][:])
+                nc.scalar.copy(out=win[t][:, :S], in_=a_ps[t][:])
             root = sb("root%d" % t, [P, 4, P], F32)
             nc.scalar.activation(out=root[:], in_=dens[t][:], func=ACT.Abs_reciprocal_sqrt, bias=0.5)
             sq = sb("sq%d" % t, [P, 4, P], F32)
-            nc.scalar.activation(out=sq[:], in_=root[:], func=ACT.Square)
+            if t in SQ_V:
+                nc.vector.tensor_tensor(out=sq[:], in0=root[:], in1=root[:], op=ALU.mult)
+            else:
+                nc.scalar.activation(out=sq[:], in_=root[:], func=ACT.Square)
             r = bank(4 + t, "inv%d" % t, [P, S])
             for c in range(4):
                 nc.tensor.transpose(r[:, P * c : P * (c + 1)], sq[:, c, :], ident[:])
             inv.append(r)
             if t < 2:
-                a_sb[t + 2] = sb("a_sb%d" % (t + 2), [P, S], F32, a_tags[t + 2])
-                nc.scalar.copy(out=a_sb[t + 2][:], in_=a_ps[t + 2][:])
+                nc.scalar.copy(out=win[t + 2][:, :S], in_=a_ps[t + 2][:])
 
         out_rows = out.rearrange("(p t) n -> t p n", t=PACK)
         for t in range(PACK):
             a6 = sb("a6_%d" % t, [P, S], F32)
-            for h in range(2):
-                gather(a6, a_sb[t], l6, h, t == 3 or (t == 2 and h == 1))
+            gather_row(a6, win[t], l6, t, A6_S)
             diff = sb("diff%d" % t, [P, S], F32)
             nc.vector.tensor_tensor(out=diff[:], in0=a_ps[t][:], in1=a6[:], op=ALU.subtract)
             res = sb("res%d" % t, [P, S], F32)
-            nc.vector.tensor_tensor(out=res[:], in0=inv[t][:], in1=diff[:], op=ALU.mult)
-            nc.sync.dma_start(out_rows[t], res[:])
+            parts = 2 if t == PACK - 1 else 1
+            for h in range(parts):
+                cols = slice(S // parts * h, S // parts * (h + 1))
+                nc.vector.tensor_tensor(out=res[:, cols], in0=inv[t][:, cols], in1=diff[:, cols], op=ALU.mult)
+                nc.sync.dma_start(out_rows[t][:, cols], res[:, cols])

@@ -20,9 +20,14 @@ P = 128
 PACK = 4
 HALF = S // 2
 LCOLS = HALF // 16
-SQ_V = (0, 1, 2)
+SQ_V = (0, 1)
+SQ_G = (2, 3)
+S7_S = 0
+PA_V = 1
+ODDS_G = 0
+DIFF_G = (0, 1)
 A6_S = 4
-E5_S = 1
+E5_S = 3
 
 
 def tile_picked_forknormbfoldodds_none_p_kernel(tc, x_words, x_scales, w1, gn, w2, gm, w3, offs, n1, n2, n3, n4, n5, n6, n7, out):
@@ -60,6 +65,12 @@ def tile_picked_forknormbfoldodds_none_p_kernel(tc, x_words, x_scales, w1, gn, w
                 nc.scalar.activation(out=dst, in_=src, func=ACT.Copy)
             else:
                 nc.vector.tensor_copy(out=dst, in_=src)
+
+        def deal_gpsimd(raw, grouped):
+            dst = grouped[:].rearrange("p (t m j) -> p t m j", t=PACK, j=PACK)
+            src = raw[:].rearrange("p j (m t) -> p t m j", t=PACK)
+            for t in range(PACK):
+                nc.gpsimd.tensor_scalar(out=dst[:, t], in0=src[:, t], scalar1=1.0, scalar2=0.0, op0=ALU.mult, op1=ALU.add)
 
         def quantize(codes, scales, grouped, c0, c1):
             nc.vector.quantize_mx(out=codes[:, c0:c1].bitcast(FP8X4), scales=scales[:, c0:c1], in_=grouped[:, PACK * c0 : PACK * c1])
@@ -136,9 +147,10 @@ def tile_picked_forknormbfoldodds_none_p_kernel(tc, x_words, x_scales, w1, gn, w
             nc.scalar.activation(out=win[t][:, :S], in_=y_ps[t][:], func=ACT.Exp, scale=0.5)
 
         w3_g = sb("w3_g", [P, PACK * N], BF16)
-        w3_c = sb("w3_c", [P, N], U32)
+        deal_gpsimd(w3_raw, w3_g)
+        w2_g = sb("w2_g", [P, PACK * N], BF16)
+        deal_gpsimd(w2_raw, w2_g)
         w3_s = sb("w3_s", [P, N], U8)
-        w2_c = sb("w2_c", [P, N], U32)
         w2_s = sb("w2_s", [P, N], U8)
 
         odds = []
@@ -167,10 +179,9 @@ def tile_picked_forknormbfoldodds_none_p_kernel(tc, x_words, x_scales, w1, gn, w
             nc.scalar.activation(out=ln_top[:], in_=top[:], func=ACT.Ln)
             nc.scalar.activation(out=ln_bot[:], in_=bot[:], func=ACT.Ln)
             odds.append(sb("odds%d" % t, [P, 4, P], F32))
-            nc.vector.tensor_tensor(out=odds[t][:], in0=ln_top[:], in1=ln_bot[:], op=ALU.subtract)
+            (nc.gpsimd if t < ODDS_G else nc.vector).tensor_tensor(out=odds[t][:], in0=ln_top[:], in1=ln_bot[:], op=ALU.subtract)
             if t == 1:
-                for m0 in range(0, P, 32):
-                    deal(w3_raw, w3_g, m0, m0 + 32, False)
+                w3_c = sb("w3_c", [P, N], U32, "e3_1")
                 quantize(w3_c, w3_s, w3_g, 0, N)
 
         back = [bank(3 - c, "back%d" % c, [P, PACK, P]) for c in range(4)]
@@ -193,17 +204,18 @@ def tile_picked_forknormbfoldodds_none_p_kernel(tc, x_words, x_scales, w1, gn, w
             for t in range(PACK):
                 product(b_ps[t], w3_c, w3_s, t, z2_c, z2_s, HALF * h, HALF * (h + 1))
 
-        w2_g = sb("w2_g", [P, PACK * N], BF16, "ln_top3")
-        for m0 in range(0, P, 32):
-            deal(w2_raw, w2_g, m0, m0 + 32, False)
+        w2_c = sb("w2_c", [P, N], U32, "odds3")
         quantize(w2_c, w2_s, w2_g, 0, N)
         z_planes = sb("z_planes", [P, PACK, S], BF16)
         gates = sb("gates", [P, PACK, W], F32, "ln_bot3")
         for t in range(PACK):
-            pa = sb("pa%d" % t, [P, W], F32)
+            pa = sb("pa%d" % t, [P, W], F32, "ln_top3" if t < PA_V else None)
             gate = gates[:, t, :]
             nc.scalar.activation(out=gate, in_=ds[t][:].indirect(l2[:]), func=ACT.Sigmoid)
-            nc.scalar.activation(out=pa[:], in_=ds[t][:].indirect(l1[:]), func=ACT.Copy)
+            if t < PA_V:
+                nc.vector.tensor_copy(out=pa[:], in_=ds[t][:].indirect(l1[:]))
+            else:
+                nc.scalar.activation(out=pa[:], in_=ds[t][:].indirect(l1[:]), func=ACT.Copy)
             nc.vector.tensor_tensor(out=ds[t][:].indirect(l2[:]), in0=pa[:], in1=gate, op=ALU.mult)
             nc.vector.tensor_scalar(out=z_planes[:, t, :], in0=ds[t][:], scalar1=gn_sb[:, t : t + 1], scalar2=None, op0=ALU.mult)
         dens = []
@@ -211,7 +223,7 @@ def tile_picked_forknormbfoldodds_none_p_kernel(tc, x_words, x_scales, w1, gn, w
             size = win[t]
             nc.scalar.activation(out=size[:, :S], in_=b_ps[t][:], func=ACT.Abs)
             s7 = sb("s7_%d" % t, [P, S], F32)
-            gather_row(s7, size, l7, t, 0)
+            gather_row(s7, size, l7, 3 - t, S7_S)
             den = bank(4 + t, "den%d" % t, [P, 4, P])
             for c in range(4):
                 cols = slice(P * c, P * (c + 1))
@@ -239,7 +251,9 @@ def tile_picked_forknormbfoldodds_none_p_kernel(tc, x_words, x_scales, w1, gn, w
             root = sb("root%d" % t, [P, 4, P], F32)
             nc.scalar.activation(out=root[:], in_=dens[t][:], func=ACT.Abs_reciprocal_sqrt, bias=0.5)
             sq = sb("sq%d" % t, [P, 4, P], F32)
-            if t in SQ_V:
+            if t in SQ_G:
+                nc.gpsimd.tensor_tensor(out=sq[:], in0=root[:], in1=root[:], op=ALU.mult)
+            elif t in SQ_V:
                 nc.vector.tensor_tensor(out=sq[:], in0=root[:], in1=root[:], op=ALU.mult)
             else:
                 nc.scalar.activation(out=sq[:], in_=root[:], func=ACT.Square)
@@ -255,7 +269,10 @@ def tile_picked_forknormbfoldodds_none_p_kernel(tc, x_words, x_scales, w1, gn, w
             a6 = sb("a6_%d" % t, [P, S], F32)
             gather_row(a6, win[t], l6, t, A6_S)
             diff = sb("diff%d" % t, [P, S], F32)
-            nc.vector.tensor_tensor(out=diff[:], in0=a_ps[t][:], in1=a6[:], op=ALU.subtract)
+            if t in DIFF_G:
+                nc.gpsimd.tensor_tensor(out=diff[:], in0=win[t][:, :S], in1=a6[:], op=ALU.subtract)
+            else:
+                nc.vector.tensor_tensor(out=diff[:], in0=a_ps[t][:], in1=a6[:], op=ALU.subtract)
             res = sb("res%d" % t, [P, S], F32)
             parts = 2 if t == PACK - 1 else 1
             for h in range(parts):

@@ -17,17 +17,18 @@ ACT = mybir.ActivationFunctionType
 ALU = mybir.AluOpType
 
 P = 128
-PACK = 4
+SLOTS = 4
+LAST = SLOTS - 1
 HALF = S // 2
-LCOLS = HALF // 16
-SQ_V = (0, 1)
-SQ_G = (2, 3)
-S7_S = 0
-PA_V = 1
-ODDS_G = 0
-DIFF_G = (0, 1)
-A6_S = 4
-E5_S = 3
+HALF_COLS = HALF // 16
+CHUNKS = S // P
+
+W1_ON_VECTOR = 56
+WHOLE_ROW_TILES = 2
+N5_ON_VECTOR = 1
+Y_COPIES_ON_SCALAR = 3
+PA_ON_VECTOR = 2
+SQUARES_ON_GPSIMD = 2
 
 
 def tile_picked_forknormbfoldodds_none_p_kernel(tc, x_words, x_scales, w1, gn, w2, gm, w3, offs, n1, n2, n3, n4, n5, n6, n7, out):
@@ -37,245 +38,272 @@ def tile_picked_forknormbfoldodds_none_p_kernel(tc, x_words, x_scales, w1, gn, w
         keep = ctx.enter_context(tc.tile_pool(name="keep", bufs=1))
         psum = ctx.enter_context(tc.psum_pool(name="psum", bufs=1))
 
-        def sb(name, shape, dtype, tag=None):
-            return keep.tile(shape, dtype, name=name, tag=tag or name, align_bytes=64)
+        def sb(name, shape, dtype, after=None):
+            return keep.tile(shape, dtype, name=name, tag=after or name, align_bytes=64)
 
         def bank(index, name, shape):
             return psum.tile(shape, F32, name=name, tag="bank%d" % index)
 
         def load_list(name, src):
-            tl = lists.tile([P, src.shape[1]], U16, name=name)
-            nc.sync.dma_start(tl[:], src)
-            return tl
+            offsets = lists.tile([P, src.shape[1]], U16, name=name)
+            nc.sync.dma_start(offsets[:], src)
+            return offsets
 
-        def load_weight(name, src, tag):
-            raw = sb(name, [P, PACK, H], F32, tag)
-            nc.sync.dma_start(raw[:], src.rearrange("(p j) n -> p j n", j=PACK))
+        def load_weight(name, src, after):
+            raw = sb(name, [P, SLOTS, H], F32, after)
+            nc.sync.dma_start(raw[:], src.rearrange("(p j) n -> p j n", j=SLOTS))
             return raw
 
-        def load_gain(name, src, tag):
-            g = sb(name, [P, PACK], F32, tag)
-            nc.sync.dma_start(g[:], src.rearrange("(p t) o -> p (t o)", t=PACK))
-            return g
+        def load_gain(name, src, after):
+            gain = sb(name, [P, SLOTS], F32, after)
+            nc.sync.dma_start(gain[:], src.rearrange("(p t) o -> p (t o)", t=SLOTS))
+            return gain
 
-        def deal(raw, grouped, m0, m1, on_scalar):
-            dst = grouped[:].rearrange("p (t m j) -> p m j t", t=PACK, j=PACK)[:, m0:m1]
-            src = raw[:].rearrange("p j (m t) -> p m j t", t=PACK)[:, m0:m1]
-            if on_scalar:
-                nc.scalar.activation(out=dst, in_=src, func=ACT.Copy)
-            else:
-                nc.vector.tensor_copy(out=dst, in_=src)
-
-        def deal_gpsimd(raw, grouped):
-            dst = grouped[:].rearrange("p (t m j) -> p t m j", t=PACK, j=PACK)
-            src = raw[:].rearrange("p j (m t) -> p t m j", t=PACK)
-            for t in range(PACK):
+        def deal_on_gpsimd(raw, dealt):
+            dst = dealt[:].rearrange("p (t m j) -> p t m j", t=SLOTS, j=SLOTS)
+            src = raw[:].rearrange("p j (m t) -> p t m j", t=SLOTS)
+            for t in range(SLOTS):
                 nc.gpsimd.tensor_scalar(out=dst[:, t], in0=src[:, t], scalar1=1.0, scalar2=0.0, op0=ALU.mult, op1=ALU.add)
 
-        def quantize(codes, scales, grouped, c0, c1):
-            nc.vector.quantize_mx(out=codes[:, c0:c1].bitcast(FP8X4), scales=scales[:, c0:c1], in_=grouped[:, PACK * c0 : PACK * c1])
+        def quantize(words, scales, values, c0, c1):
+            nc.vector.quantize_mx(out=words[:, c0:c1].bitcast(FP8X4), scales=scales[:, c0:c1], in_=values[:, SLOTS * c0 : SLOTS * c1])
 
-        def product(acc, w_codes, w_scales, t, codes, scales, c0, c1):
-            nc.tensor.matmul_mx(
-                out=acc[:, c0:c1],
-                lhsT=w_codes[:, P * t : P * (t + 1)].bitcast(FP8X4),
-                lhsT_scale=w_scales[:, P * t : P * (t + 1)],
-                rhs=codes[:, c0:c1].bitcast(FP8X4),
-                rhs_scale=scales[:, c0:c1],
-                start=True,
-                stop=True,
-            )
+        def product(result, w_words, w_scales, words, scales):
+            for t in range(SLOTS):
+                for h in range(2):
+                    places = slice(HALF * h, HALF * (h + 1))
+                    nc.tensor.matmul_mx(
+                        out=result[t][:, places],
+                        lhsT=w_words[:, P * t : P * (t + 1)].bitcast(FP8X4),
+                        lhsT_scale=w_scales[:, P * t : P * (t + 1)],
+                        rhs=words[:, places].bitcast(FP8X4),
+                        rhs_scale=scales[:, places],
+                        start=True,
+                        stop=True,
+                    )
 
-        def gather(dst, window, lst, h, on_scalar, halves=1):
-            o = dst[:, HALF * h : HALF * (h + halves)]
-            src = window[:].indirect(lst[:, LCOLS * h : LCOLS * (h + halves)])
+        def look_up(dst, window, offsets, on_scalar):
             if on_scalar:
-                nc.scalar.activation(out=o, in_=src, func=ACT.Copy)
+                nc.scalar.activation(out=dst, in_=window[:].indirect(offsets), func=ACT.Copy)
             else:
-                nc.vector.tensor_copy(out=o, in_=src)
+                nc.vector.tensor_copy(out=dst, in_=window[:].indirect(offsets))
 
-        def gather_row(dst, window, lst, t, scalar_from):
-            if 2 * t + 1 == scalar_from:
-                gather(dst, window, lst, 0, False)
-                gather(dst, window, lst, 1, True)
-            else:
-                gather(dst, window, lst, 0, 2 * t >= scalar_from, 2)
+        def look_up_halves(dst, window, offsets, h, halves, on_scalar):
+            look_up(dst[:, HALF * h : HALF * (h + halves)], window, offsets[:, HALF_COLS * h : HALF_COLS * (h + halves)], on_scalar)
 
-        x_sc = sb("x_sc", [P, T], U8)
-        nc.gpsimd.memset(x_sc[:].bitcast(I32), 0)
-        w1_raw = load_weight("w1_raw", w1, "w1_raw")
+        def add_turned(dst, first, second):
+            nc.tensor.matmul(dst, first, ident[:], is_transpose=True, start=True, stop=False)
+            nc.tensor.matmul(dst, second, ident[:], is_transpose=True, start=False, stop=True)
+
+        x_bytes = sb("x_bytes", [P, T], U8)
+        nc.gpsimd.memset(x_bytes[:].bitcast(I32), 0)
+        w1_raw = load_weight("w1_raw", w1, None)
         l_offs = load_list("l_offs", offs)
         l3 = load_list("l3", n3)
         l4 = load_list("l4", n4)
         l5 = load_list("l5", n5)
         l1 = load_list("l1", n1)
         l2 = load_list("l2", n2)
-        x_w = sb("x_w", [P, T], U32)
-        nc.sync.dma_start(x_w[:].bitcast(I32), x_words[0].rearrange("p n r -> p (n r)").bitcast(I32))
+        x_packed = sb("x_packed", [P, T], U32)
+        nc.sync.dma_start(x_packed[:].bitcast(I32), x_words[0].rearrange("p n r -> p (n r)").bitcast(I32))
         for q in range(4):
-            nc.scalar.dma_start(x_sc[32 * q : 32 * q + 4, :].bitcast(I32), x_scales[0, 4 * q : 4 * q + 4, :].bitcast(I32))
+            nc.scalar.dma_start(x_bytes[32 * q : 32 * q + 4, :].bitcast(I32), x_scales[0, 4 * q : 4 * q + 4, :].bitcast(I32))
         l7 = load_list("l7", n7)
         l6 = load_list("l6", n6)
 
         ident = sb("ident", [P, P], F32)
         make_identity(nc, ident[:])
-        win = [sb("win%d" % t, [P, 2 * S], F32) for t in range(PACK)]
-        for t in range(PACK):
-            nc.gpsimd.memset(win[t][:, S:], 0.0)
+        rows = [sb("rows%d" % t, [P, 2 * S], F32) for t in range(SLOTS)]
+        for t in range(SLOTS):
+            nc.gpsimd.memset(rows[t][:, S:], 0.0)
 
-        xg_sc = sb("xg_sc", [P, S], U8)
-        nc.vector.tensor_copy(out=xg_sc[:], in_=x_sc[:].indirect(l_offs[:]))
-        w1_g = sb("w1_g", [P, PACK * H], BF16)
-        deal(w1_raw, w1_g, 0, 56, False)
-        deal(w1_raw, w1_g, 56, 128, True)
-        w1_c = sb("w1_c", [P, H], U32, "x_sc")
-        w1_s = sb("w1_s", [P, H], U8)
-        quantize(w1_c, w1_s, w1_g, 0, H)
+        picked_bytes = sb("picked_bytes", [P, S], U8)
+        nc.vector.tensor_copy(out=picked_bytes[:], in_=x_bytes[:].indirect(l_offs[:]))
+        w1_dealt = sb("w1_dealt", [P, SLOTS * H], BF16)
+        w1_dst = w1_dealt[:].rearrange("p (t m j) -> p m j t", t=SLOTS, j=SLOTS)
+        w1_src = w1_raw[:].rearrange("p j (m t) -> p m j t", t=SLOTS)
+        nc.vector.tensor_copy(out=w1_dst[:, :W1_ON_VECTOR], in_=w1_src[:, :W1_ON_VECTOR])
+        nc.scalar.activation(out=w1_dst[:, W1_ON_VECTOR:], in_=w1_src[:, W1_ON_VECTOR:], func=ACT.Copy)
+        w1_words = sb("w1_words", [P, H], U32, "x_bytes")
+        w1_scales = sb("w1_scales", [P, H], U8)
+        quantize(w1_words, w1_scales, w1_dealt, 0, H)
         w3_raw = load_weight("w3_raw", w3, "w1_raw")
-        xg_w = sb("xg_w", [P, S], U32, "w1_g")
-        y_ps = [bank(t, "y_ps%d" % t, [P, S]) for t in range(PACK)]
+        picked_words = sb("picked_words", [P, S], U32, "w1_dealt")
+        y_psum = [bank(t, "y_psum%d" % t, [P, S]) for t in range(SLOTS)]
         for h in range(2):
-            gather(xg_w, x_w, l_offs, h, False)
-            for t in range(PACK):
-                product(y_ps[t], w1_c, w1_s, t, xg_w, xg_sc, HALF * h, HALF * (h + 1))
+            look_up_halves(picked_words, x_packed, l_offs, h, 1, False)
+        product(y_psum, w1_words, w1_scales, picked_words, picked_bytes)
 
-        w2_raw = load_weight("w2_raw", w2, "w1_g")
-        gm_sb = load_gain("gm_sb", gm, "w1_s")
-        gn_sb = load_gain("gn_sb", gn, "xg_sc")
-        ds = [sb("ds%d" % t, [P, S], F32) for t in range(PACK)]
-        for t in range(PACK):
-            nc.scalar.activation(out=win[t][:, :S], in_=y_ps[t][:], func=ACT.Exp, scale=0.5)
+        w2_raw = load_weight("w2_raw", w2, "w1_dealt")
+        gm_sb = load_gain("gm_sb", gm, "w1_scales")
+        gn_sb = load_gain("gn_sb", gn, "picked_bytes")
+        ds = [sb("ds%d" % t, [P, S], F32) for t in range(SLOTS)]
+        for t in range(SLOTS):
+            nc.scalar.activation(out=rows[t][:, :S], in_=y_psum[t][:], func=ACT.Exp, scale=0.5)
 
-        w3_g = sb("w3_g", [P, PACK * N], BF16)
-        deal_gpsimd(w3_raw, w3_g)
-        w2_g = sb("w2_g", [P, PACK * N], BF16)
-        deal_gpsimd(w2_raw, w2_g)
-        w3_s = sb("w3_s", [P, N], U8)
-        w2_s = sb("w2_s", [P, N], U8)
+        w3_dealt = sb("w3_dealt", [P, SLOTS * N], BF16)
+        deal_on_gpsimd(w3_raw, w3_dealt)
+        w2_dealt = sb("w2_dealt", [P, SLOTS * N], BF16)
+        deal_on_gpsimd(w2_raw, w2_dealt)
+        w3_scales = sb("w3_scales", [P, N], U8)
+        w2_scales = sb("w2_scales", [P, N], U8)
 
-        odds = []
-        got = []
-        for t in range(PACK):
-            e3 = sb("e3_%d" % t, [P, S], F32)
-            e4 = sb("e4_%d" % t, [P, S], F32)
-            e5 = sb("e5_%d" % t, [P, S], F32)
-            got.append((e3, e4, e5))
-            gather_row(e3, win[t], l3, t, 8)
-            gather_row(e4, win[t], l4, t, 8)
-            gather_row(e5, win[t], l5, t, E5_S)
-        for t in range(PACK):
-            nc.scalar.copy(out=ds[t][:], in_=y_ps[t][:])
-        for t in range(PACK):
-            e3, e4, e5 = got[t]
-            top = bank((4 + 2 * t) % 8, "top%d" % t, [P, 4, P])
-            bot = bank((5 + 2 * t) % 8, "bot%d" % t, [P, 4, P])
-            for acc, first, second in ((top, e3, win[t]), (bot, e5, e4)):
-                for c in range(4):
-                    cols = slice(P * c, P * (c + 1))
-                    nc.tensor.matmul(acc[:, c, :], first[:, cols], ident[:], is_transpose=True, start=True, stop=False)
-                    nc.tensor.matmul(acc[:, c, :], second[:, cols], ident[:], is_transpose=True, start=False, stop=True)
-            ln_top = sb("ln_top%d" % t, [P, 4, P], F32)
-            ln_bot = sb("ln_bot%d" % t, [P, 4, P], F32)
-            nc.scalar.activation(out=ln_top[:], in_=top[:], func=ACT.Ln)
-            nc.scalar.activation(out=ln_bot[:], in_=bot[:], func=ACT.Ln)
-            odds.append(sb("odds%d" % t, [P, 4, P], F32))
-            (nc.gpsimd if t < ODDS_G else nc.vector).tensor_tensor(out=odds[t][:], in0=ln_top[:], in1=ln_bot[:], op=ALU.subtract)
-            if t == 1:
-                w3_c = sb("w3_c", [P, N], U32, "e3_1")
-                quantize(w3_c, w3_s, w3_g, 0, N)
+        ex3 = [sb("ex3_%d" % t, [P, S], F32) for t in range(SLOTS)]
+        ex4 = [sb("ex4_%d" % t, [P, S], F32) for t in range(SLOTS)]
+        ex5 = [sb("ex5_%d" % t, [P, S], F32) for t in range(SLOTS)]
+        whole, halved = range(WHOLE_ROW_TILES), range(WHOLE_ROW_TILES, SLOTS)
+        for t, h, halves in [(t, 0, 2) for t in whole] + [(t, h, 1) for h in range(2) for t in halved]:
+            look_up_halves(ex3[t], rows[t], l3, h, halves, False)
+            look_up_halves(ex4[t], rows[t], l4, h, halves, False)
+            look_up_halves(ex5[t], rows[t], l5, h, halves, t >= N5_ON_VECTOR)
+        for t in range(SLOTS):
+            if t < Y_COPIES_ON_SCALAR:
+                nc.scalar.copy(out=ds[t][:], in_=y_psum[t][:])
+            else:
+                nc.vector.tensor_copy(out=ds[t][:], in_=y_psum[t][:])
 
-        back = [bank(3 - c, "back%d" % c, [P, PACK, P]) for c in range(4)]
-        for c in range(4):
-            for t in range(PACK):
-                nc.tensor.transpose(back[c][:, t, :], odds[t][:, c, :], ident[:])
-        z2_g = sb("z2_g", [P, PACK * S], BF16)
-        z2_c = sb("z2_c", [P, S], U32)
-        z2_s = sb("z2_s", [P, S], U8)
-        b_ps = [bank(4 + t, "b_ps%d" % t, [P, S]) for t in range(PACK)]
+        sums_bank = {(t, h): SLOTS + 2 * t + h for t in whole for h in range(2)}
+        for t in halved:
+            sums_bank[t, 0] = t - WHOLE_ROW_TILES
+            sums_bank[t, 1] = sums_bank[t - WHOLE_ROW_TILES, 0]
+        sums = {}
+
+        def add_pairs(t, h):
+            sums[t, h] = bank(sums_bank[t, h], "sums%d_%d" % (t, h), [P, 2, 2, P])
+            for side, first, second in ((0, ex3[t], rows[t]), (1, ex5[t], ex4[t])):
+                for c in range(2):
+                    places = slice(HALF * h + P * c, HALF * h + P * (c + 1))
+                    add_turned(sums[t, h][:, side, c, :], first[:, places], second[:, places])
+
+        odds = {}
+
+        def log_odds(t, h):
+            logs = sb("logs%d_%d" % (t, h), [P, 2, 2, P], F32)
+            nc.scalar.activation(out=logs[:], in_=sums[t, h][:], func=ACT.Ln)
+            odds[t, h] = sb("odds%d_%d" % (t, h), [P, 2, P], F32)
+            nc.gpsimd.tensor_tensor(out=odds[t, h][:], in0=logs[:, 0], in1=logs[:, 1], op=ALU.subtract)
+
+        for t, h in [(t, h) for t in whole for h in range(2)] + [(t, 0) for t in halved]:
+            add_pairs(t, h)
+        for t in whole:
+            log_odds(t, 0)
+        w3_words = sb("w3_words", [P, N], U32, "ex3_1")
+        quantize(w3_words, w3_scales, w3_dealt, 0, N)
+        for t in halved:
+            add_pairs(t, 1)
+        for t in halved:
+            log_odds(t, 0)
+        for t in range(SLOTS):
+            log_odds(t, 1)
+
+        z2_values = sb("z2_values", [P, SLOTS * S], BF16)
+        z2_words = sb("z2_words", [P, S], U32)
+        z2_scales = sb("z2_scales", [P, S], U8)
+        back = [bank(c, "back%d" % c, [P, SLOTS, P]) for c in range(CHUNKS)]
+        b_bank = [sums_bank[t, 1] for t in range(SLOTS)]
+        b_psum = [bank(b_bank[t], "b_psum%d" % t, [P, S]) for t in range(SLOTS)]
         for h in range(2):
             for c in (2 * h, 2 * h + 1):
+                for t in range(SLOTS):
+                    nc.tensor.transpose(back[c][:, t, :], odds[t, h][:, c % 2, :], ident[:])
                 nc.vector.tensor_tensor(
-                    out=z2_g[:, PACK * P * c : PACK * P * (c + 1)].rearrange("p (j t) -> p j t", t=PACK),
+                    out=z2_values[:, SLOTS * P * c : SLOTS * P * (c + 1)].rearrange("p (j t) -> p j t", t=SLOTS),
                     in0=back[c][:].rearrange("p t j -> p j t"),
-                    in1=gm_sb[:].unsqueeze(1).to_broadcast([P, P, PACK]),
+                    in1=gm_sb[:].unsqueeze(1).to_broadcast([P, P, SLOTS]),
                     op=ALU.mult,
                 )
-            quantize(z2_c, z2_s, z2_g, HALF * h, HALF * (h + 1))
-            for t in range(PACK):
-                product(b_ps[t], w3_c, w3_s, t, z2_c, z2_s, HALF * h, HALF * (h + 1))
+            quantize(z2_words, z2_scales, z2_values, HALF * h, HALF * (h + 1))
+        product(b_psum, w3_words, w3_scales, z2_words, z2_scales)
 
-        w2_c = sb("w2_c", [P, N], U32, "odds3")
-        quantize(w2_c, w2_s, w2_g, 0, N)
-        z_planes = sb("z_planes", [P, PACK, S], BF16)
-        gates = sb("gates", [P, PACK, W], F32, "ln_bot3")
-        for t in range(PACK):
-            pa = sb("pa%d" % t, [P, W], F32, "ln_top3" if t < PA_V else None)
-            gate = gates[:, t, :]
-            nc.scalar.activation(out=gate, in_=ds[t][:].indirect(l2[:]), func=ACT.Sigmoid)
-            if t < PA_V:
-                nc.vector.tensor_copy(out=pa[:], in_=ds[t][:].indirect(l1[:]))
-            else:
-                nc.scalar.activation(out=pa[:], in_=ds[t][:].indirect(l1[:]), func=ACT.Copy)
-            nc.vector.tensor_tensor(out=ds[t][:].indirect(l2[:]), in0=pa[:], in1=gate, op=ALU.mult)
-            nc.vector.tensor_scalar(out=z_planes[:, t, :], in0=ds[t][:], scalar1=gn_sb[:, t : t + 1], scalar2=None, op0=ALU.mult)
+        w2_words = sb("w2_words", [P, N], U32, "logs2_1")
+        quantize(w2_words, w2_scales, w2_dealt, 0, N)
+
+        z_values = sb("z_values", [P, SLOTS * S], BF16)
+        z_slots = sb("z_slots", [P, SLOTS, S], BF16)
+        ra = sb("ra", [P, SLOTS, W], F32)
+        gates = sb("gates", [P, SLOTS, W], F32, "logs3_1")
+        pa_after = ("ex3_2", "ex4_3")
+        for t in range(SLOTS):
+            pa = sb("pa%d" % t, [P, W], F32, pa_after[t] if t < PA_ON_VECTOR else None)
+            nc.scalar.activation(out=gates[:, t, :], in_=ds[t][:].indirect(l2[:]), func=ACT.Sigmoid)
+            look_up(pa[:], ds[t], l1[:], t >= PA_ON_VECTOR)
+            nc.gpsimd.tensor_tensor(out=ra[:, t, :], in0=pa[:], in1=gates[:, t, :], op=ALU.mult)
+        for t in range(SLOTS):
+            nc.vector.tensor_copy(out=ds[t][:].indirect(l2[:]), in_=ra[:, t, :])
+            engine = nc.gpsimd if t < LAST else nc.vector
+            engine.tensor_scalar(out=z_slots[:, t, :], in0=ds[t][:], scalar1=gn_sb[:, t : t + 1], scalar2=0.0, op0=ALU.mult, op1=ALU.add)
+
         dens = []
-        for t in range(PACK):
-            size = win[t]
-            nc.scalar.activation(out=size[:, :S], in_=b_ps[t][:], func=ACT.Abs)
-            s7 = sb("s7_%d" % t, [P, S], F32)
-            gather_row(s7, size, l7, 3 - t, S7_S)
-            den = bank(4 + t, "den%d" % t, [P, 4, P])
-            for c in range(4):
-                cols = slice(P * c, P * (c + 1))
-                nc.tensor.matmul(den[:, c, :], s7[:, cols], ident[:], is_transpose=True, start=True, stop=False)
-                nc.tensor.matmul(den[:, c, :], size[:, cols], ident[:], is_transpose=True, start=False, stop=True)
+
+        def denominator(t):
+            nc.scalar.activation(out=rows[t][:, :S], in_=b_psum[t][:], func=ACT.Abs)
+            size7 = sb("size7_%d" % t, [P, S], F32, "z_values" if t == LAST else None)
+            look_up_halves(size7, rows[t], l7, 0, 2, t < LAST)
+            den = bank(b_bank[t], "den%d" % t, [P, CHUNKS, P])
+            for c in range(CHUNKS):
+                places = slice(P * c, P * (c + 1))
+                add_turned(den[:, c, :], size7[:, places], rows[t][:, places])
             dens.append(den)
 
-        z_g = sb("z_g", [P, PACK * S], BF16)
-        z_c = sb("z_c", [P, S], U32, "s7_2")
-        z_s = sb("z_s", [P, S], U8)
-        a_ps = [bank(t, "a_ps%d" % t, [P, S]) for t in range(PACK)]
+        for t in range(LAST):
+            denominator(t)
+
+        z_words = sb("z_words", [P, S], U32)
+        z_scales = sb("z_scales", [P, S], U8)
+        a_psum = [bank(t, "a_psum%d" % t, [P, S]) for t in range(SLOTS)]
         for h in range(2):
             nc.vector.tensor_copy(
-                out=z_g[:, PACK * HALF * h : PACK * HALF * (h + 1)].rearrange("p (c i t) -> p c t i", i=4, t=PACK),
-                in_=z_planes[:, :, HALF * h : HALF * (h + 1)].rearrange("p t (c i) -> p c t i", i=4),
+                out=z_values[:, SLOTS * HALF * h : SLOTS * HALF * (h + 1)].rearrange("p (c i t) -> p c t i", i=4, t=SLOTS),
+                in_=z_slots[:, :, HALF * h : HALF * (h + 1)].rearrange("p t (c i) -> p c t i", i=4),
             )
-            quantize(z_c, z_s, z_g, HALF * h, HALF * (h + 1))
-            for t in range(PACK):
-                product(a_ps[t], w2_c, w2_s, t, z_c, z_s, HALF * h, HALF * (h + 1))
+            quantize(z_words, z_scales, z_values, HALF * h, HALF * (h + 1))
+        product(a_psum, w2_words, w2_scales, z_words, z_scales)
 
-        inv = []
-        for t in range(PACK):
-            if t < 2:
-                nc.scalar.copy(out=win[t][:, :S], in_=a_ps[t][:])
-            root = sb("root%d" % t, [P, 4, P], F32)
-            nc.scalar.activation(out=root[:], in_=dens[t][:], func=ACT.Abs_reciprocal_sqrt, bias=0.5)
-            sq = sb("sq%d" % t, [P, 4, P], F32)
-            if t in SQ_G:
-                nc.gpsimd.tensor_tensor(out=sq[:], in0=root[:], in1=root[:], op=ALU.mult)
-            elif t in SQ_V:
-                nc.vector.tensor_tensor(out=sq[:], in0=root[:], in1=root[:], op=ALU.mult)
-            else:
-                nc.scalar.activation(out=sq[:], in_=root[:], func=ACT.Square)
-            r = bank(4 + t, "inv%d" % t, [P, S])
-            for c in range(4):
-                nc.tensor.transpose(r[:, P * c : P * (c + 1)], sq[:, c, :], ident[:])
-            inv.append(r)
-            if t < 2:
-                nc.scalar.copy(out=win[t + 2][:, :S], in_=a_ps[t + 2][:])
+        denominator(LAST)
 
-        out_rows = out.rearrange("(p t) n -> t p n", t=PACK)
-        for t in range(PACK):
-            a6 = sb("a6_%d" % t, [P, S], F32)
-            gather_row(a6, win[t], l6, t, A6_S)
-            diff = sb("diff%d" % t, [P, S], F32)
-            if t in DIFF_G:
-                nc.gpsimd.tensor_tensor(out=diff[:], in0=win[t][:, :S], in1=a6[:], op=ALU.subtract)
+        roots = [sb("root%d" % t, [P, CHUNKS, P], F32) for t in range(SLOTS)]
+        inverse = []
+
+        def inverse_root(t):
+            nc.scalar.activation(out=roots[t][:], in_=dens[t][:], func=ACT.Abs_reciprocal_sqrt, bias=0.5)
+
+        def square_and_turn(t):
+            square = sb("square%d" % t, [P, CHUNKS, P], F32, "z_slots" if t == 0 else None)
+            if t < SQUARES_ON_GPSIMD:
+                nc.gpsimd.tensor_tensor(out=square[:], in0=roots[t][:], in1=roots[t][:], op=ALU.mult)
             else:
-                nc.vector.tensor_tensor(out=diff[:], in0=a_ps[t][:], in1=a6[:], op=ALU.subtract)
-            res = sb("res%d" % t, [P, S], F32)
-            parts = 2 if t == PACK - 1 else 1
-            for h in range(parts):
-                cols = slice(S // parts * h, S // parts * (h + 1))
-                nc.vector.tensor_tensor(out=res[:, cols], in0=inv[t][:, cols], in1=diff[:, cols], op=ALU.mult)
-                nc.sync.dma_start(out_rows[t][:, cols], res[:, cols])
+                nc.scalar.activation(out=square[:], in_=roots[t][:], func=ACT.Square)
+            inv = bank(b_bank[t], "inverse%d" % t, [P, S])
+            for c in range(CHUNKS):
+                nc.tensor.transpose(inv[:, P * c : P * (c + 1)], square[:, c, :], ident[:])
+            inverse.append(inv)
+
+        for t in range(LAST):
+            inverse_root(t)
+        for t in range(SLOTS):
+            nc.scalar.copy(out=rows[t][:, :S], in_=a_psum[t][:])
+        inverse_root(LAST)
+        for t in range(SLOTS):
+            square_and_turn(t)
+
+        out_tiles = out.rearrange("(p t) n -> t p n", t=SLOTS)
+        diffs = [sb("diff%d" % t, [P, S], F32) for t in range(SLOTS)]
+
+        def finish(t, places):
+            nc.vector.tensor_tensor(out=results[t][:, places], in0=inverse[t][:, places], in1=diffs[t][:, places], op=ALU.mult)
+            nc.sync.dma_start(out_tiles[t][:, places], results[t][:, places])
+
+        a6 = [sb("a6_%d" % t, [P, S], F32) for t in range(SLOTS)]
+        results = [sb("result%d" % t, [P, S], F32) for t in range(SLOTS)]
+        half_places = [slice(HALF * h, HALF * (h + 1)) for h in range(2)]
+        for t in range(LAST):
+            look_up_halves(a6[t], rows[t], l6, 0, 2, False)
+            nc.gpsimd.tensor_tensor(out=diffs[t][:], in0=rows[t][:, :S], in1=a6[t][:], op=ALU.subtract)
+        for t in range(LAST - 1):
+            finish(t, slice(0, S))
+        for h in range(2):
+            look_up_halves(a6[LAST], rows[LAST], l6, h, 1, True)
+            nc.vector.tensor_tensor(out=diffs[LAST][:, half_places[h]], in0=a_psum[LAST][:, half_places[h]], in1=a6[LAST][:, half_places[h]], op=ALU.subtract)
+            finish(LAST, half_places[h])
+        for h in range(2):
+            finish(LAST - 1, half_places[h])

from contextlib import ExitStack

import concourse.mybir as mybir
from concourse.masks import make_identity

K, T, S, N, H, W = 512, 2048, 512, 512, 512, 256
FLOPS = 2 * K * H * S + 2 * 2 * H * N * S

F32 = mybir.dt.float32
BF16 = mybir.dt.bfloat16
I32 = mybir.dt.int32
U32 = mybir.dt.uint32
U16 = mybir.dt.uint16
U8 = mybir.dt.uint8
FP8X4 = mybir.dt.float8_e4m3fn_x4
ACT = mybir.ActivationFunctionType
ALU = mybir.AluOpType

P = 128
SLOTS = 4
LAST = SLOTS - 1
HALF = S // 2
HALF_COLS = HALF // 16
CHUNKS = S // P

W1_ON_VECTOR = 56
WHOLE_ROW_TILES = 2
N5_ON_VECTOR = 1
Y_COPIES_ON_SCALAR = 3
PA_ON_VECTOR = 2
SQUARES_ON_GPSIMD = 2


def tile_picked_forknormbfoldodds_none_p_kernel(tc, x_words, x_scales, w1, gn, w2, gm, w3, offs, n1, n2, n3, n4, n5, n6, n7, out):
    nc = tc.nc
    with ExitStack() as ctx:
        lists = ctx.enter_context(tc.tile_pool(name="lists", bufs=1))
        keep = ctx.enter_context(tc.tile_pool(name="keep", bufs=1))
        psum = ctx.enter_context(tc.psum_pool(name="psum", bufs=1))

        def sb(name, shape, dtype, after=None):
            return keep.tile(shape, dtype, name=name, tag=after or name, align_bytes=64)

        def bank(index, name, shape):
            return psum.tile(shape, F32, name=name, tag="bank%d" % index)

        def load_list(name, src):
            offsets = lists.tile([P, src.shape[1]], U16, name=name)
            nc.sync.dma_start(offsets[:], src)
            return offsets

        def load_weight(name, src, after):
            raw = sb(name, [P, SLOTS, H], F32, after)
            nc.sync.dma_start(raw[:], src.rearrange("(p j) n -> p j n", j=SLOTS))
            return raw

        def load_gain(name, src, after):
            gain = sb(name, [P, SLOTS], F32, after)
            nc.sync.dma_start(gain[:], src.rearrange("(p t) o -> p (t o)", t=SLOTS))
            return gain

        def deal_on_gpsimd(raw, dealt):
            dst = dealt[:].rearrange("p (t m j) -> p t m j", t=SLOTS, j=SLOTS)
            src = raw[:].rearrange("p j (m t) -> p t m j", t=SLOTS)
            for t in range(SLOTS):
                nc.gpsimd.tensor_scalar(out=dst[:, t], in0=src[:, t], scalar1=1.0, scalar2=0.0, op0=ALU.mult, op1=ALU.add)

        def quantize(words, scales, values, c0, c1):
            nc.vector.quantize_mx(out=words[:, c0:c1].bitcast(FP8X4), scales=scales[:, c0:c1], in_=values[:, SLOTS * c0 : SLOTS * c1])

        def product(result, w_words, w_scales, words, scales):
            for t in range(SLOTS):
                for h in range(2):
                    places = slice(HALF * h, HALF * (h + 1))
                    nc.tensor.matmul_mx(
                        out=result[t][:, places],
                        lhsT=w_words[:, P * t : P * (t + 1)].bitcast(FP8X4),
                        lhsT_scale=w_scales[:, P * t : P * (t + 1)],
                        rhs=words[:, places].bitcast(FP8X4),
                        rhs_scale=scales[:, places],
                        start=True,
                        stop=True,
                    )

        def look_up(dst, window, offsets, on_scalar):
            if on_scalar:
                nc.scalar.activation(out=dst, in_=window[:].indirect(offsets), func=ACT.Copy)
            else:
                nc.vector.tensor_copy(out=dst, in_=window[:].indirect(offsets))

        def look_up_halves(dst, window, offsets, h, halves, on_scalar):
            look_up(dst[:, HALF * h : HALF * (h + halves)], window, offsets[:, HALF_COLS * h : HALF_COLS * (h + halves)], on_scalar)

        def add_turned(dst, first, second):
            nc.tensor.matmul(dst, first, ident[:], is_transpose=True, start=True, stop=False)
            nc.tensor.matmul(dst, second, ident[:], is_transpose=True, start=False, stop=True)

        x_bytes = sb("x_bytes", [P, T], U8)
        nc.gpsimd.memset(x_bytes[:].bitcast(I32), 0)
        w1_raw = load_weight("w1_raw", w1, None)
        l_offs = load_list("l_offs", offs)
        l3 = load_list("l3", n3)
        l4 = load_list("l4", n4)
        l5 = load_list("l5", n5)
        l1 = load_list("l1", n1)
        l2 = load_list("l2", n2)
        x_packed = sb("x_packed", [P, T], U32)
        nc.sync.dma_start(x_packed[:].bitcast(I32), x_words[0].rearrange("p n r -> p (n r)").bitcast(I32))
        for q in range(4):
            nc.scalar.dma_start(x_bytes[32 * q : 32 * q + 4, :].bitcast(I32), x_scales[0, 4 * q : 4 * q + 4, :].bitcast(I32))
        l7 = load_list("l7", n7)
        l6 = load_list("l6", n6)

        ident = sb("ident", [P, P], F32)
        make_identity(nc, ident[:])
        rows = [sb("rows%d" % t, [P, 2 * S], F32) for t in range(SLOTS)]
        for t in range(SLOTS):
            nc.gpsimd.memset(rows[t][:, S:], 0.0)

        picked_bytes = sb("picked_bytes", [P, S], U8)
        nc.vector.tensor_copy(out=picked_bytes[:], in_=x_bytes[:].indirect(l_offs[:]))
        w1_dealt = sb("w1_dealt", [P, SLOTS * H], BF16)
        w1_dst = w1_dealt[:].rearrange("p (t m j) -> p m j t", t=SLOTS, j=SLOTS)
        w1_src = w1_raw[:].rearrange("p j (m t) -> p m j t", t=SLOTS)
        nc.vector.tensor_copy(out=w1_dst[:, :W1_ON_VECTOR], in_=w1_src[:, :W1_ON_VECTOR])
        nc.scalar.activation(out=w1_dst[:, W1_ON_VECTOR:], in_=w1_src[:, W1_ON_VECTOR:], func=ACT.Copy)
        w1_words = sb("w1_words", [P, H], U32, "x_bytes")
        w1_scales = sb("w1_scales", [P, H], U8)
        quantize(w1_words, w1_scales, w1_dealt, 0, H)
        w3_raw = load_weight("w3_raw", w3, "w1_raw")
        picked_words = sb("picked_words", [P, S], U32, "w1_dealt")
        y_psum = [bank(t, "y_psum%d" % t, [P, S]) for t in range(SLOTS)]
        for h in range(2):
            look_up_halves(picked_words, x_packed, l_offs, h, 1, False)
        product(y_psum, w1_words, w1_scales, picked_words, picked_bytes)

        w2_raw = load_weight("w2_raw", w2, "w1_dealt")
        gm_sb = load_gain("gm_sb", gm, "w1_scales")
        gn_sb = load_gain("gn_sb", gn, "picked_bytes")
        ds = [sb("ds%d" % t, [P, S], F32) for t in range(SLOTS)]
        for t in range(SLOTS):
            nc.scalar.activation(out=rows[t][:, :S], in_=y_psum[t][:], func=ACT.Exp, scale=0.5)

        w3_dealt = sb("w3_dealt", [P, SLOTS * N], BF16)
        deal_on_gpsimd(w3_raw, w3_dealt)
        w2_dealt = sb("w2_dealt", [P, SLOTS * N], BF16)
        deal_on_gpsimd(w2_raw, w2_dealt)
        w3_scales = sb("w3_scales", [P, N], U8)
        w2_scales = sb("w2_scales", [P, N], U8)

        ex3 = [sb("ex3_%d" % t, [P, S], F32) for t in range(SLOTS)]
        ex4 = [sb("ex4_%d" % t, [P, S], F32) for t in range(SLOTS)]
        ex5 = [sb("ex5_%d" % t, [P, S], F32) for t in range(SLOTS)]
        whole, halved = range(WHOLE_ROW_TILES), range(WHOLE_ROW_TILES, SLOTS)
        for t, h, halves in [(t, 0, 2) for t in whole] + [(t, h, 1) for h in range(2) for t in halved]:
            look_up_halves(ex3[t], rows[t], l3, h, halves, False)
            look_up_halves(ex4[t], rows[t], l4, h, halves, False)
            look_up_halves(ex5[t], rows[t], l5, h, halves, t >= N5_ON_VECTOR)
        for t in range(SLOTS):
            if t < Y_COPIES_ON_SCALAR:
                nc.scalar.copy(out=ds[t][:], in_=y_psum[t][:])
            else:
                nc.vector.tensor_copy(out=ds[t][:], in_=y_psum[t][:])

        sums_bank = {(t, h): SLOTS + 2 * t + h for t in whole for h in range(2)}
        for t in halved:
            sums_bank[t, 0] = t - WHOLE_ROW_TILES
            sums_bank[t, 1] = sums_bank[t - WHOLE_ROW_TILES, 0]
        sums = {}

        def add_pairs(t, h):
            sums[t, h] = bank(sums_bank[t, h], "sums%d_%d" % (t, h), [P, 2, 2, P])
            for side, first, second in ((0, ex3[t], rows[t]), (1, ex5[t], ex4[t])):
                for c in range(2):
                    places = slice(HALF * h + P * c, HALF * h + P * (c + 1))
                    add_turned(sums[t, h][:, side, c, :], first[:, places], second[:, places])

        odds = {}

        def log_odds(t, h):
            logs = sb("logs%d_%d" % (t, h), [P, 2, 2, P], F32)
            nc.scalar.activation(out=logs[:], in_=sums[t, h][:], func=ACT.Ln)
            odds[t, h] = sb("odds%d_%d" % (t, h), [P, 2, P], F32)
            nc.gpsimd.tensor_tensor(out=odds[t, h][:], in0=logs[:, 0], in1=logs[:, 1], op=ALU.subtract)

        for t, h in [(t, h) for t in whole for h in range(2)] + [(t, 0) for t in halved]:
            add_pairs(t, h)
        for t in whole:
            log_odds(t, 0)
        w3_words = sb("w3_words", [P, N], U32, "ex3_1")
        quantize(w3_words, w3_scales, w3_dealt, 0, N)
        for t in halved:
            add_pairs(t, 1)
        for t in halved:
            log_odds(t, 0)
        for t in range(SLOTS):
            log_odds(t, 1)

        z2_values = sb("z2_values", [P, SLOTS * S], BF16)
        z2_words = sb("z2_words", [P, S], U32)
        z2_scales = sb("z2_scales", [P, S], U8)
        back = [bank(c, "back%d" % c, [P, SLOTS, P]) for c in range(CHUNKS)]
        b_bank = [sums_bank[t, 1] for t in range(SLOTS)]
        b_psum = [bank(b_bank[t], "b_psum%d" % t, [P, S]) for t in range(SLOTS)]
        for h in range(2):
            for c in (2 * h, 2 * h + 1):
                for t in range(SLOTS):
                    nc.tensor.transpose(back[c][:, t, :], odds[t, h][:, c % 2, :], ident[:])
                nc.vector.tensor_tensor(
                    out=z2_values[:, SLOTS * P * c : SLOTS * P * (c + 1)].rearrange("p (j t) -> p j t", t=SLOTS),
                    in0=back[c][:].rearrange("p t j -> p j t"),
                    in1=gm_sb[:].unsqueeze(1).to_broadcast([P, P, SLOTS]),
                    op=ALU.mult,
                )
            quantize(z2_words, z2_scales, z2_values, HALF * h, HALF * (h + 1))
        product(b_psum, w3_words, w3_scales, z2_words, z2_scales)

        w2_words = sb("w2_words", [P, N], U32, "logs2_1")
        quantize(w2_words, w2_scales, w2_dealt, 0, N)

        z_values = sb("z_values", [P, SLOTS * S], BF16)
        z_slots = sb("z_slots", [P, SLOTS, S], BF16)
        ra = sb("ra", [P, SLOTS, W], F32)
        gates = sb("gates", [P, SLOTS, W], F32, "logs3_1")
        pa_after = ("ex3_2", "ex4_3")
        for t in range(SLOTS):
            pa = sb("pa%d" % t, [P, W], F32, pa_after[t] if t < PA_ON_VECTOR else None)
            nc.scalar.activation(out=gates[:, t, :], in_=ds[t][:].indirect(l2[:]), func=ACT.Sigmoid)
            look_up(pa[:], ds[t], l1[:], t >= PA_ON_VECTOR)
            nc.gpsimd.tensor_tensor(out=ra[:, t, :], in0=pa[:], in1=gates[:, t, :], op=ALU.mult)
        for t in range(SLOTS):
            nc.vector.tensor_copy(out=ds[t][:].indirect(l2[:]), in_=ra[:, t, :])
            engine = nc.gpsimd if t < LAST else nc.vector
            engine.tensor_scalar(out=z_slots[:, t, :], in0=ds[t][:], scalar1=gn_sb[:, t : t + 1], scalar2=0.0, op0=ALU.mult, op1=ALU.add)

        dens = []

        def denominator(t):
            nc.scalar.activation(out=rows[t][:, :S], in_=b_psum[t][:], func=ACT.Abs)
            size7 = sb("size7_%d" % t, [P, S], F32, "z_values" if t == LAST else None)
            look_up_halves(size7, rows[t], l7, 0, 2, t < LAST)
            den = bank(b_bank[t], "den%d" % t, [P, CHUNKS, P])
            for c in range(CHUNKS):
                places = slice(P * c, P * (c + 1))
                add_turned(den[:, c, :], size7[:, places], rows[t][:, places])
            dens.append(den)

        for t in range(LAST):
            denominator(t)

        z_words = sb("z_words", [P, S], U32)
        z_scales = sb("z_scales", [P, S], U8)
        a_psum = [bank(t, "a_psum%d" % t, [P, S]) for t in range(SLOTS)]
        for h in range(2):
            nc.vector.tensor_copy(
                out=z_values[:, SLOTS * HALF * h : SLOTS * HALF * (h + 1)].rearrange("p (c i t) -> p c t i", i=4, t=SLOTS),
                in_=z_slots[:, :, HALF * h : HALF * (h + 1)].rearrange("p t (c i) -> p c t i", i=4),
            )
            quantize(z_words, z_scales, z_values, HALF * h, HALF * (h + 1))
        product(a_psum, w2_words, w2_scales, z_words, z_scales)

        denominator(LAST)

        roots = [sb("root%d" % t, [P, CHUNKS, P], F32) for t in range(SLOTS)]
        inverse = []

        def inverse_root(t):
            nc.scalar.activation(out=roots[t][:], in_=dens[t][:], func=ACT.Abs_reciprocal_sqrt, bias=0.5)

        def square_and_turn(t):
            square = sb("square%d" % t, [P, CHUNKS, P], F32, "z_slots" if t == 0 else None)
            if t < SQUARES_ON_GPSIMD:
                nc.gpsimd.tensor_tensor(out=square[:], in0=roots[t][:], in1=roots[t][:], op=ALU.mult)
            else:
                nc.scalar.activation(out=square[:], in_=roots[t][:], func=ACT.Square)
            inv = bank(b_bank[t], "inverse%d" % t, [P, S])
            for c in range(CHUNKS):
                nc.tensor.transpose(inv[:, P * c : P * (c + 1)], square[:, c, :], ident[:])
            inverse.append(inv)

        for t in range(LAST):
            inverse_root(t)
        for t in range(SLOTS):
            nc.scalar.copy(out=rows[t][:, :S], in_=a_psum[t][:])
        inverse_root(LAST)
        for t in range(SLOTS):
            square_and_turn(t)

        out_tiles = out.rearrange("(p t) n -> t p n", t=SLOTS)
        diffs = [sb("diff%d" % t, [P, S], F32) for t in range(SLOTS)]

        def finish(t, places):
            nc.vector.tensor_tensor(out=results[t][:, places], in0=inverse[t][:, places], in1=diffs[t][:, places], op=ALU.mult)
            nc.sync.dma_start(out_tiles[t][:, places], results[t][:, places])

        a6 = [sb("a6_%d" % t, [P, S], F32) for t in range(SLOTS)]
        results = [sb("result%d" % t, [P, S], F32) for t in range(SLOTS)]
        half_places = [slice(HALF * h, HALF * (h + 1)) for h in range(2)]
        for t in range(LAST):
            look_up_halves(a6[t], rows[t], l6, 0, 2, False)
            nc.gpsimd.tensor_tensor(out=diffs[t][:], in0=rows[t][:, :S], in1=a6[t][:], op=ALU.subtract)
        for t in range(LAST - 1):
            finish(t, slice(0, S))
        for h in range(2):
            look_up_halves(a6[LAST], rows[LAST], l6, h, 1, True)
            nc.vector.tensor_tensor(out=diffs[LAST][:, half_places[h]], in0=a_psum[LAST][:, half_places[h]], in1=a6[LAST][:, half_places[h]], op=ALU.subtract)
            finish(LAST, half_places[h])
        for h in range(2):
            finish(LAST - 1, half_places[h])
